import numpy as np
import ml_dtypes


def mxq(x, axis, fmt="e4m3"):
    dtype, down = {"e4m3": (ml_dtypes.float8_e4m3fn, 7), "e5m2": (ml_dtypes.float8_e5m2, 14)}[fmt]
    v = np.moveaxis(np.asarray(x, np.float32).astype(ml_dtypes.bfloat16).astype(np.float64), axis, -1)
    blocks = v.reshape(v.shape[:-1] + (-1, 32))
    amax = np.abs(blocks).max(-1, keepdims=True)
    byte = np.maximum(np.where(amax > 0, np.frexp(amax)[1] - 1 + 127, 0) - down, 1)
    scale = np.exp2(byte - 127.0)
    codes = (blocks / scale).astype(np.float32).astype(dtype).astype(np.float64)
    return np.moveaxis((codes * scale).reshape(v.shape), -1, axis)


WIDE = False


def mx_kscale(k):
    if not WIDE:
        return np.ones(k)
    levels = np.array([10, -10, 5, -5, 0])
    if k % 512:
        return np.exp2(np.random.permutation(np.resize(levels, k // 32))).repeat(32)
    a = np.empty((k // 512, 16))
    for p in range(k // 512):
        a[p, :8] = np.random.permutation(np.resize(levels, 8))
        for g in range(8):
            far = levels[np.abs(levels - a[p, g]) >= 10]
            a[p, g + 8] = far[np.random.randint(len(far))]
    return np.exp2(a.ravel()).repeat(32)


def f64(x):
    return np.asarray(x).astype(np.float64)


E2M1 = np.array([0.0, 0.5, 1.0, 1.5, 2.0, 3.0, 4.0, 6.0, -0.0, -0.5, -1.0, -1.5, -2.0, -3.0, -4.0, -6.0])


def pack_weight(w, fmt):
    k, n = w.shape
    w = f64(np.asarray(w, np.float32).astype(ml_dtypes.bfloat16)).reshape(k // 32, 32, n)
    amax = np.abs(w).max(1)
    if fmt == "e4m3":
        byte = np.frexp(amax)[1] - 1 + 127 - 7
    else:
        mant, ex = np.frexp(amax / 6.0)
        byte = np.where(mant > 0.5, ex, ex - 1) + 127
    byte = np.clip(np.where(amax > 0, byte, 1), 1, 254)
    scaled = (w * np.exp2(127.0 - byte)[:, None, :]).reshape(k, n).astype(np.float32)
    by_word = np.ascontiguousarray(scaled.reshape(k // 512, 128, 4, n).transpose(0, 1, 3, 2))
    if fmt == "e4m3":
        words = by_word.astype(ml_dtypes.float8_e4m3fn).view(np.uint8)
    else:
        c = by_word.astype(ml_dtypes.float4_e2m1fn).view(np.uint8) & 0xF
        words = (c[..., 0::2] | (c[..., 1::2] << 4)).reshape(k // 512, 128, 2 * n)
    return np.ascontiguousarray(words), np.ascontiguousarray(byte.astype(np.uint8).reshape(k // 512, 16, n))


def unpack_weight(words, scales, fmt):
    g, _, n = scales.shape
    words = np.ascontiguousarray(words).reshape(g, 128, n, -1)
    if fmt == "e4m3":
        vals = words.view(ml_dtypes.float8_e4m3fn).astype(np.float64)
    else:
        nib = np.empty((g, 128, n, 4), np.uint8)
        nib[..., 0::2] = words & 0xF
        nib[..., 1::2] = words >> 4
        vals = E2M1[nib]
    vals = vals * np.repeat(np.exp2(scales.astype(np.float64) - 127.0), 8, axis=1)[..., None]
    return vals.transpose(0, 1, 3, 2).reshape(g * 512, n)


def planes(y):
    n, m = y.shape
    v = y.astype(np.float32).astype(ml_dtypes.bfloat16).astype(np.float64).reshape(n // 32, 32, m)
    top = np.abs(v).max(1)
    byte = np.clip(np.where(top > 0, np.frexp(top)[1] - 1 + 127 - 7, 1), 1, 254)
    codes = (v * np.exp2(127.0 - byte)[:, None, :]).reshape(n, m).astype(np.float32).astype(ml_dtypes.float8_e4m3fn).view(np.uint8)
    words = codes.reshape(n // 512, 128, 4, m).transpose(0, 1, 3, 2)
    return np.ascontiguousarray(words), np.ascontiguousarray(byte.astype(np.uint8).reshape(n // 512, 16, m))


O, K, M, T = 512, 1536, 1024, 1024


def setup_inputs():
    n = np.random.standard_normal
    s = mx_kscale(K)[:, None]
    x = n((K, T)); x[:O] *= 6.0
    w = n((K, M)) / np.sqrt(K) / s; w[:O] /= 2.0
    p_w8 = pack_weight(w[:O], "e4m3")
    p_w4 = pack_weight(w[O:], "e2m1")
    return {
        "x": (x * s).astype(np.float32),
        "w8_words": p_w8[0],
        "w8_scales": p_w8[1],
        "w4_words": p_w4[0],
        "w4_scales": p_w4[1],
        "g": (n((1024, 1024))).astype(np.float32),
    }


def reference(x, w8_words, w8_scales, w4_words, w4_scales, g):
    x_ = mxq(f64(x), 0, "e4m3")
    w8_ = unpack_weight(w8_words, w8_scales, "e4m3")
    w4_ = unpack_weight(w4_words, w4_scales, "e2m1")
    y = x_[:O].T @ w8_ + x_[O:].T @ w4_
    out_0 = f64(g) * y
    return (out_0,) + planes(out_0)

@@ -1,0 +1,193 @@
+from contextlib import ExitStack
+
+import concourse.mybir as mybir
+
+K, M, T = 1536, 1024, 1024
+FLOPS = 2 * K * M * T
+
+F32 = mybir.dt.float32
+BF16 = mybir.dt.bfloat16
+I32 = mybir.dt.int32
+U32 = mybir.dt.uint32
+U8 = mybir.dt.uint8
+FP8X4 = mybir.dt.float8_e4m3fn_x4
+FP4X4 = mybir.dt.float4_e2m1fn_x4
+
+P = 128
+PACK = 4
+SPAN = P * PACK
+PASSES = K // SPAN
+GROUPS = T // SPAN
+N = 512
+HALVES = M // N
+M_VECTOR = 80
+
+
+def tile_mix_outl_tm_pl_mul_kernel(
+    tc, x, w8_words, w8_scales, w4_words, w4_scales, g, out_0, out_1, out_2
+):
+    nc = tc.nc
+    with ExitStack() as ctx:
+        keep = ctx.enter_context(tc.tile_pool(name="keep", bufs=1))
+        psum = ctx.enter_context(tc.psum_pool(name="psum", bufs=1))
+        ctx.enter_context(tc.manual_schedule())
+
+        chunks = [(a, c) for a in range(GROUPS) for c in range(PASSES)]
+        x_raw = {ac: keep.tile([P, PACK, SPAN], F32, name="x_raw%d%d" % ac) for ac in chunks}
+        x_bf = {ac: keep.tile([P, PACK * SPAN], BF16, name="x_bf%d%d" % ac, align_bytes=64) for ac in chunks}
+        x_codes = {ac: keep.tile([P, SPAN], U32, name="x_codes%d%d" % ac, align_bytes=64) for ac in chunks}
+        x_scales = {ac: keep.tile([P, SPAN], U8, name="x_scales%d%d" % ac, align_bytes=64) for ac in chunks}
+        pairs = [(a, u) for a in range(GROUPS) for u in range(2)]
+        g_sb = {au: keep.tile([P, 2, M], F32, name="g%d%d" % au) for au in pairs}
+        o_sb = [keep.tile([P, PACK, M], F32, name="o%d" % a) for a in range(GROUPS)]
+        halves = [(a, h) for a in range(GROUPS) for h in range(HALVES)]
+        o_bf = {ah: keep.tile([P, N * PACK], BF16, name="o_bf%d%d" % ah, align_bytes=64) for ah in halves}
+        o_codes = [keep.tile([P, M], U32, name="o_codes%d" % a, align_bytes=64) for a in range(GROUPS)]
+        o_scales = keep.tile([P, GROUPS * M], U8, align_bytes=64)
+        w8_sb = keep.tile([P, M], U32, align_bytes=64)
+        w4_sb = keep.tile([P, 2, 2 * M], U8, align_bytes=64)
+        w_scales = keep.tile([P, PASSES * M], U8, align_bytes=64)
+
+        def load_x(a, c):
+            rows = x[c * SPAN : (c + 1) * SPAN, a * SPAN : (a + 1) * SPAN]
+            nc.sync.dma_start(out=x_raw[a, c][:], in_=rows.rearrange("(p j) t -> p j t", j=PACK))
+
+        def load_g(a, u):
+            rows = g[a * SPAN : (a + 1) * SPAN, :].rearrange("(p r) n -> p r n", r=PACK)
+            nc.sync.dma_start(out=g_sb[a, u][:], in_=rows[:, 2 * u : 2 * u + 2, :])
+
+        def load_scales(src, first):
+            count = src.shape[0]
+            dst = w_scales[:, first * M : (first + count) * M].bitcast(I32).rearrange("p (a n) -> p a n", a=count)
+            for q in range(4):
+                rows = src[:, 4 * q : 4 * q + 4, :].bitcast(I32).rearrange("a r n -> r a n")
+                nc.sync.dma_start(out=dst[32 * q : 32 * q + 4], in_=rows)
+
+        def deal_views(a, c):
+            src = x_raw[a, c][:].rearrange("p j (m r) -> p m j r", r=PACK)
+            dst = x_bf[a, c][:].rearrange("p (r m j) -> p m j r", r=PACK, j=PACK)
+            return dst, src
+
+        def round_x_vector(a, c):
+            dst, src = deal_views(a, c)
+            nc.vector.tensor_copy(out=dst[:, :M_VECTOR], in_=src[:, :M_VECTOR])
+
+        def round_x_scalar(a, c):
+            dst, src = deal_views(a, c)
+            nc.scalar.copy(out=dst[:, M_VECTOR:], in_=src[:, M_VECTOR:])
+
+        def quantize_x(a, c):
+            nc.vector.quantize_mx(out=x_codes[a, c][:].bitcast(FP8X4), scales=x_scales[a, c][:], in_=x_bf[a, c][:])
+
+        order = [(0, 0), (0, 1), (1, 0), (1, 1), (2, 0), (3, 0), (2, 1), (3, 1)]
+        acc = {}
+
+        def multiply(a, c):
+            for r, h in order:
+                if c == 0:
+                    acc[r, h] = psum.tile([P, N], F32, name="acc%d%d" % (r, h))
+                if c == 0:
+                    rhs = w8_sb[:, h * N : (h + 1) * N].bitcast(FP8X4)
+                else:
+                    rhs = w4_sb[:, c - 1, 2 * h * N : 2 * (h + 1) * N].bitcast(FP4X4)
+                nc.tensor.matmul_mx(
+                    out=acc[r, h][:],
+                    lhsT=x_codes[a, c][:, r * P : (r + 1) * P].bitcast(FP8X4),
+                    lhsT_scale=x_scales[a, c][:, r * P : (r + 1) * P],
+                    rhs=rhs,
+                    rhs_scale=w_scales[:, c * M + h * N : c * M + (h + 1) * N],
+                    start=(c == 0),
+                    stop=(c == PASSES - 1),
+                )
+
+        def gate(a, tiles):
+            for r, h in tiles:
+                cols = slice(h * N, (h + 1) * N)
+                nc.vector.tensor_tensor(
+                    out=o_sb[a][:, r, cols], in0=acc[r, h][:], in1=g_sb[a, r // 2][:, r % 2, cols], op=mybir.AluOpType.mult
+                )
+
+        def out_views(a, h):
+            src = o_sb[a][:, :, h * N : (h + 1) * N].rearrange("p r n -> p n r")
+            dst = o_bf[a, h][:].rearrange("p (n r) -> p n r", r=PACK)
+            return dst, src
+
+        def round_out_scalar(a, h):
+            dst, src = out_views(a, h)
+            nc.scalar.copy(out=dst, in_=src)
+
+        def round_out_vector(a, h):
+            dst, src = out_views(a, h)
+            nc.vector.tensor_copy(out=dst, in_=src)
+
+        def quantize_out(a, h):
+            nc.vector.quantize_mx(
+                out=o_codes[a][:, h * N : (h + 1) * N].bitcast(FP8X4),
+                scales=o_scales[:, a * M + h * N : a * M + (h + 1) * N],
+                in_=o_bf[a, h][:],
+            )
+
+        def store_out(a, r0, r1):
+            rows = out_0[a * SPAN : (a + 1) * SPAN, :].rearrange("(p r) n -> p r n", r=PACK)
+            nc.sync.dma_start(out=rows[:, r0:r1, :], in_=o_sb[a][:, r0:r1, :])
+
+        def store_codes(a):
+            nc.sync.dma_start(out=out_1[a].rearrange("p n i -> p (n i)").bitcast(I32), in_=o_codes[a][:].bitcast(I32))
+
+        def store_scales():
+            src = o_scales[:].bitcast(I32).rearrange("p (a n) -> p a n", a=GROUPS)
+            for q in range(4):
+                rows = out_2[:, 4 * q : 4 * q + 4, :].bitcast(I32).rearrange("a r n -> r a n")
+                nc.sync.dma_start(out=rows, in_=src[32 * q : 32 * q + 4])
+
+        nc.vector.memset(w_scales[:].bitcast(I32), 0)
+        load_x(0, 0)
+        nc.sync.dma_start(out=w8_sb[:].bitcast(I32), in_=w8_words[0].rearrange("p n i -> p (n i)").bitcast(I32))
+        load_scales(w8_scales, 0)
+        load_x(0, 1)
+        nc.sync.dma_start(out=w4_sb[:].bitcast(I32), in_=w4_words.bitcast(I32).rearrange("a p n -> p a n"))
+        load_scales(w4_scales, 1)
+        load_x(0, 2)
+        load_g(0, 0)
+        load_g(0, 1)
+        for c in range(PASSES):
+            load_x(1, c)
+        load_g(1, 0)
+        load_g(1, 1)
+
+        for c in range(PASSES):
+            round_x_vector(0, c)
+            round_x_scalar(0, c)
+            quantize_x(0, c)
+            multiply(0, c)
+        gate(0, order)
+        store_out(0, 0, PACK)
+
+        round_x_vector(1, 0)
+        round_x_scalar(1, 0)
+        quantize_x(1, 0)
+        multiply(1, 0)
+        round_out_scalar(0, 0)
+        round_x_vector(1, 1)
+        round_x_scalar(1, 1)
+        quantize_x(1, 1)
+        multiply(1, 1)
+        round_x_vector(1, 2)
+        round_x_scalar(1, 2)
+        quantize_out(0, 0)
+        quantize_x(1, 2)
+        multiply(1, 2)
+        round_out_scalar(0, 1)
+        gate(1, order[:4])
+        store_out(1, 0, 2)
+        gate(1, order[4:6])
+        round_out_scalar(1, 0)
+        gate(1, order[6:])
+        store_out(1, 2, PACK)
+        round_out_vector(1, 1)
+        quantize_out(0, 1)
+        store_codes(0)
+        quantize_out(1, 0)
+        quantize_out(1, 1)
+        store_scales()
+        store_codes(1)

@@ -20,7 +20,8 @@ PASSES = K // SPAN
 GROUPS = T // SPAN
 N = 512
 HALVES = M // N
-M_VECTOR = 80
+W8_ROW = 4
+OUT_ROW = (8, 12)
 
 
 def tile_mix_outl_tm_pl_mul_kernel(
@@ -33,8 +34,13 @@ def tile_mix_outl_tm_pl_mul_kernel(
         ctx.enter_context(tc.manual_schedule())
 
         chunks = [(a, c) for a in range(GROUPS) for c in range(PASSES)]
-        x_raw = {ac: keep.tile([P, PACK, SPAN], F32, name="x_raw%d%d" % ac) for ac in chunks}
-        x_bf = {ac: keep.tile([P, PACK * SPAN], BF16, name="x_bf%d%d" % ac, align_bytes=64) for ac in chunks}
+        x_whole = [keep.tile([P, PACK, T], F32, name="x_whole%d" % c) for c in range(PASSES - 1)]
+        x_last = [keep.tile([P, PACK, SPAN], F32, name="x_last%d" % a) for a in range(GROUPS)]
+        x_bf = {
+            (a, c, u): keep.tile([P, 2 * SPAN], BF16, name="x_bf%d%d%d" % (a, c, u), align_bytes=64)
+            for a, c in chunks
+            for u in range(2)
+        }
         x_codes = {ac: keep.tile([P, SPAN], U32, name="x_codes%d%d" % ac, align_bytes=64) for ac in chunks}
         x_scales = {ac: keep.tile([P, SPAN], U8, name="x_scales%d%d" % ac, align_bytes=64) for ac in chunks}
         pairs = [(a, u) for a in range(GROUPS) for u in range(2)]
@@ -43,59 +49,70 @@ def tile_mix_outl_tm_pl_mul_kernel(
         halves = [(a, h) for a in range(GROUPS) for h in range(HALVES)]
         o_bf = {ah: keep.tile([P, N * PACK], BF16, name="o_bf%d%d" % ah, align_bytes=64) for ah in halves}
         o_codes = [keep.tile([P, M], U32, name="o_codes%d" % a, align_bytes=64) for a in range(GROUPS)]
-        o_scales = keep.tile([P, GROUPS * M], U8, align_bytes=64)
+        o_scales = [keep.tile([P, M], U8, name="o_scales%d" % a, align_bytes=64) for a in range(GROUPS)]
         w8_sb = keep.tile([P, M], U32, align_bytes=64)
         w4_sb = keep.tile([P, 2, 2 * M], U8, align_bytes=64)
-        w_scales = keep.tile([P, PASSES * M], U8, align_bytes=64)
+        w8_plane = keep.tile([P, M], U8, align_bytes=64)
+        w4_planes = keep.tile([P, 2 * M], U8, align_bytes=64)
 
-        def load_x(a, c):
-            rows = x[c * SPAN : (c + 1) * SPAN, a * SPAN : (a + 1) * SPAN]
-            nc.sync.dma_start(out=x_raw[a, c][:], in_=rows.rearrange("(p j) t -> p j t", j=PACK))
+        def load_x_whole(c):
+            rows = x[c * SPAN : (c + 1) * SPAN, :]
+            nc.sync.dma_start(out=x_whole[c][:], in_=rows.rearrange("(p j) t -> p j t", j=PACK))
+
+        def load_x_last(a):
+            rows = x[(PASSES - 1) * SPAN :, a * SPAN : (a + 1) * SPAN]
+            nc.sync.dma_start(out=x_last[a][:], in_=rows.rearrange("(p j) t -> p j t", j=PACK))
 
         def load_g(a, u):
             rows = g[a * SPAN : (a + 1) * SPAN, :].rearrange("(p r) n -> p r n", r=PACK)
             nc.sync.dma_start(out=g_sb[a, u][:], in_=rows[:, 2 * u : 2 * u + 2, :])
 
-        def load_scales(src, first):
-            count = src.shape[0]
-            dst = w_scales[:, first * M : (first + count) * M].bitcast(I32).rearrange("p (a n) -> p a n", a=count)
-            for q in range(4):
-                rows = src[:, 4 * q : 4 * q + 4, :].bitcast(I32).rearrange("a r n -> r a n")
-                nc.sync.dma_start(out=dst[32 * q : 32 * q + 4], in_=rows)
+        def load_scales(planes, src, first_row):
+            dst = planes[:].bitcast(I32).rearrange("p (a n) -> p a n", a=src.shape[0])
+            for s in range(4):
+                rows = src[:, s:16:4, :].bitcast(I32).rearrange("a q n -> q a n")
+                nc.sync.dma_start(out=dst[first_row + s : P : 32], in_=rows)
 
-        def deal_views(a, c):
-            src = x_raw[a, c][:].rearrange("p j (m r) -> p m j r", r=PACK)
-            dst = x_bf[a, c][:].rearrange("p (r m j) -> p m j r", r=PACK, j=PACK)
+        def deal_views(a, c, u):
+            raw = x_last[a][:] if c == PASSES - 1 else x_whole[c][:, :, a * SPAN : (a + 1) * SPAN]
+            src = raw.rearrange("p j (m r) -> p m j r", r=PACK)[:, :, :, 2 * u : 2 * u + 2]
+            dst = x_bf[a, c, u][:].rearrange("p (r m j) -> p m j r", r=2, j=PACK)
             return dst, src
 
-        def round_x_vector(a, c):
-            dst, src = deal_views(a, c)
-            nc.vector.tensor_copy(out=dst[:, :M_VECTOR], in_=src[:, :M_VECTOR])
+        def round_x_vector(a, c, u):
+            dst, src = deal_views(a, c, u)
+            nc.vector.tensor_copy(out=dst, in_=src)
 
-        def round_x_scalar(a, c):
-            dst, src = deal_views(a, c)
-            nc.scalar.copy(out=dst[:, M_VECTOR:], in_=src[:, M_VECTOR:])
+        def round_x_scalar(a, c, u):
+            dst, src = deal_views(a, c, u)
+            nc.scalar.copy(out=dst, in_=src)
 
         def quantize_x(a, c):
-            nc.vector.quantize_mx(out=x_codes[a, c][:].bitcast(FP8X4), scales=x_scales[a, c][:], in_=x_bf[a, c][:])
+            for u in range(2):
+                cols = slice(2 * u * P, 2 * (u + 1) * P)
+                nc.vector.quantize_mx(
+                    out=x_codes[a, c][:, cols].bitcast(FP8X4), scales=x_scales[a, c][:, cols], in_=x_bf[a, c, u][:]
+                )
 
         order = [(0, 0), (0, 1), (1, 0), (1, 1), (2, 0), (3, 0), (2, 1), (3, 1)]
         acc = {}
 
-        def multiply(a, c):
-            for r, h in order:
+        def multiply(a, c, tiles):
+            for r, h in tiles:
+                cols = slice(h * N, (h + 1) * N)
                 if c == 0:
-                    acc[r, h] = psum.tile([P, N], F32, name="acc%d%d" % (r, h))
-                if c == 0:
-                    rhs = w8_sb[:, h * N : (h + 1) * N].bitcast(FP8X4)
+                    acc[a, r, h] = psum.tile([P, N], F32, name="acc%d%d" % (r, h))
+                    rhs = w8_sb[:, cols].bitcast(FP8X4)
+                    rhs_scale = w8_plane[W8_ROW:, cols]
                 else:
                     rhs = w4_sb[:, c - 1, 2 * h * N : 2 * (h + 1) * N].bitcast(FP4X4)
+                    rhs_scale = w4_planes[:, (c - 1) * M + h * N : (c - 1) * M + (h + 1) * N]
                 nc.tensor.matmul_mx(
-                    out=acc[r, h][:],
+                    out=acc[a, r, h][:],
                     lhsT=x_codes[a, c][:, r * P : (r + 1) * P].bitcast(FP8X4),
                     lhsT_scale=x_scales[a, c][:, r * P : (r + 1) * P],
                     rhs=rhs,
-                    rhs_scale=w_scales[:, c * M + h * N : c * M + (h + 1) * N],
+                    rhs_scale=rhs_scale,
                     start=(c == 0),
                     stop=(c == PASSES - 1),
                 )
@@ -104,13 +121,15 @@ def tile_mix_outl_tm_pl_mul_kernel(
             for r, h in tiles:
                 cols = slice(h * N, (h + 1) * N)
                 nc.vector.tensor_tensor(
-                    out=o_sb[a][:, r, cols], in0=acc[r, h][:], in1=g_sb[a, r // 2][:, r % 2, cols], op=mybir.AluOpType.mult
+                    out=o_sb[a][:, r, cols], in0=acc[a, r, h][:], in1=g_sb[a, r // 2][:, r % 2, cols], op=mybir.AluOpType.mult
                 )
 
         def out_views(a, h):
-            src = o_sb[a][:, :, h * N : (h + 1) * N].rearrange("p r n -> p n r")
-            dst = o_bf[a, h][:].rearrange("p (n r) -> p n r", r=PACK)
-            return dst, src
+            rows = o_sb[a][:, :, h * N : (h + 1) * N]
+            if h == 0:
+                return o_bf[a, h][:].rearrange("p (n r) -> p n r", r=PACK), rows.rearrange("p r n -> p n r")
+            dst = o_bf[a, h][:].rearrange("p (c i r) -> p c r i", i=4, r=PACK)
+            return dst, rows.rearrange("p r (c i) -> p c r i", i=4)
 
         def round_out_scalar(a, h):
             dst, src = out_views(a, h)
@@ -123,7 +142,7 @@ def tile_mix_outl_tm_pl_mul_kernel(
         def quantize_out(a, h):
             nc.vector.quantize_mx(
                 out=o_codes[a][:, h * N : (h + 1) * N].bitcast(FP8X4),
-                scales=o_scales[:, a * M + h * N : a * M + (h + 1) * N],
+                scales=o_scales[a][OUT_ROW[a] :, h * N : (h + 1) * N],
                 in_=o_bf[a, h][:],
             )
 
@@ -134,60 +153,60 @@ def tile_mix_outl_tm_pl_mul_kernel(
         def store_codes(a):
             nc.sync.dma_start(out=out_1[a].rearrange("p n i -> p (n i)").bitcast(I32), in_=o_codes[a][:].bitcast(I32))
 
-        def store_scales():
-            src = o_scales[:].bitcast(I32).rearrange("p (a n) -> p a n", a=GROUPS)
-            for q in range(4):
-                rows = out_2[:, 4 * q : 4 * q + 4, :].bitcast(I32).rearrange("a r n -> r a n")
-                nc.sync.dma_start(out=rows, in_=src[32 * q : 32 * q + 4])
+        def store_scales(a, queue):
+            src = o_scales[a][:].bitcast(I32)
+            for s in range(4):
+                queue.dma_start(out=out_2[a, s:16:4, :].bitcast(I32), in_=src[OUT_ROW[a] + s : P : 32])
 
-        nc.vector.memset(w_scales[:].bitcast(I32), 0)
-        load_x(0, 0)
+        nc.vector.memset(w8_plane[:].bitcast(I32), 0)
+        nc.vector.memset(w4_planes[:].bitcast(I32), 0)
+        load_x_whole(0)
         nc.sync.dma_start(out=w8_sb[:].bitcast(I32), in_=w8_words[0].rearrange("p n i -> p (n i)").bitcast(I32))
-        load_scales(w8_scales, 0)
-        load_x(0, 1)
+        load_scales(w8_plane, w8_scales, W8_ROW)
+        load_x_whole(1)
         nc.sync.dma_start(out=w4_sb[:].bitcast(I32), in_=w4_words.bitcast(I32).rearrange("a p n -> p a n"))
-        load_scales(w4_scales, 1)
-        load_x(0, 2)
-        load_g(0, 0)
-        load_g(0, 1)
-        for c in range(PASSES):
-            load_x(1, c)
-        load_g(1, 0)
-        load_g(1, 1)
+        load_scales(w4_planes, w4_scales, 0)
+        for a in range(GROUPS):
+            load_x_last(a)
+            load_g(a, 0)
+            load_g(a, 1)
 
-        for c in range(PASSES):
-            round_x_vector(0, c)
-            round_x_scalar(0, c)
-            quantize_x(0, c)
-            multiply(0, c)
-        gate(0, order)
-        store_out(0, 0, PACK)
-
-        round_x_vector(1, 0)
-        round_x_scalar(1, 0)
-        quantize_x(1, 0)
-        multiply(1, 0)
-        round_out_scalar(0, 0)
-        round_x_vector(1, 1)
-        round_x_scalar(1, 1)
-        quantize_x(1, 1)
-        multiply(1, 1)
-        round_x_vector(1, 2)
-        round_x_scalar(1, 2)
-        quantize_out(0, 0)
-        quantize_x(1, 2)
-        multiply(1, 2)
+        for c in range(PASSES - 1):
+            for a in range(GROUPS):
+                round_x_vector(a, c, 0)
+                round_x_scalar(a, c, 1)
+            for a in range(GROUPS):
+                quantize_x(a, c)
+            multiply(0, c, order)
+        round_x_vector(0, 2, 0)
+        round_x_scalar(0, 2, 1)
+        quantize_x(0, 2)
+        multiply(0, 2, order)
+        for i, tile in enumerate(order):
+            gate(0, [tile])
+            multiply(1, 0, [tile])
+            multiply(1, 1, [tile])
+            if i == 5:
+                round_out_scalar(0, 0)
         round_out_scalar(0, 1)
-        gate(1, order[:4])
+        store_out(0, 0, PACK)
+        round_x_vector(1, 2, 0)
+        round_x_vector(1, 2, 1)
+        quantize_x(1, 2)
+        multiply(1, 2, order)
+        quantize_out(0, 0)
+        gate(1, order[:2])
+        quantize_out(0, 1)
+        store_codes(0)
+        store_scales(0, nc.sync)
+        gate(1, order[2:4])
         store_out(1, 0, 2)
         gate(1, order[4:6])
         round_out_scalar(1, 0)
         gate(1, order[6:])
         store_out(1, 2, PACK)
         round_out_vector(1, 1)
-        quantize_out(0, 1)
-        store_codes(0)
-        quantize_out(1, 0)
         quantize_out(1, 1)
-        store_scales()
+        quantize_out(1, 0)
         store_codes(1)
+        store_scales(1, nc.sync)

from contextlib import ExitStack

import concourse.mybir as mybir

K, M, T = 1536, 1024, 1024
FLOPS = 2 * K * M * T

F32 = mybir.dt.float32
BF16 = mybir.dt.bfloat16
I32 = mybir.dt.int32
U32 = mybir.dt.uint32
U8 = mybir.dt.uint8
FP8X4 = mybir.dt.float8_e4m3fn_x4
FP4X4 = mybir.dt.float4_e2m1fn_x4

P = 128
PACK = 4
SPAN = P * PACK
PASSES = K // SPAN
GROUPS = T // SPAN
N = 512
HALVES = M // N
W8_ROW = 4
OUT_ROW = (8, 12)


def tile_mix_outl_tm_pl_mul_kernel(
    tc, x, w8_words, w8_scales, w4_words, w4_scales, g, out_0, out_1, out_2
):
    nc = tc.nc
    with ExitStack() as ctx:
        keep = ctx.enter_context(tc.tile_pool(name="keep", bufs=1))
        psum = ctx.enter_context(tc.psum_pool(name="psum", bufs=1))
        ctx.enter_context(tc.manual_schedule())

        chunks = [(a, c) for a in range(GROUPS) for c in range(PASSES)]
        x_whole = [keep.tile([P, PACK, T], F32, name="x_whole%d" % c) for c in range(PASSES - 1)]
        x_last = [keep.tile([P, PACK, SPAN], F32, name="x_last%d" % a) for a in range(GROUPS)]
        x_bf = {
            (a, c, u): keep.tile([P, 2 * SPAN], BF16, name="x_bf%d%d%d" % (a, c, u), align_bytes=64)
            for a, c in chunks
            for u in range(2)
        }
        x_codes = {ac: keep.tile([P, SPAN], U32, name="x_codes%d%d" % ac, align_bytes=64) for ac in chunks}
        x_scales = {ac: keep.tile([P, SPAN], U8, name="x_scales%d%d" % ac, align_bytes=64) for ac in chunks}
        pairs = [(a, u) for a in range(GROUPS) for u in range(2)]
        g_sb = {au: keep.tile([P, 2, M], F32, name="g%d%d" % au) for au in pairs}
        o_sb = [keep.tile([P, PACK, M], F32, name="o%d" % a) for a in range(GROUPS)]
        halves = [(a, h) for a in range(GROUPS) for h in range(HALVES)]
        o_bf = {ah: keep.tile([P, N * PACK], BF16, name="o_bf%d%d" % ah, align_bytes=64) for ah in halves}
        o_codes = [keep.tile([P, M], U32, name="o_codes%d" % a, align_bytes=64) for a in range(GROUPS)]
        o_scales = [keep.tile([P, M], U8, name="o_scales%d" % a, align_bytes=64) for a in range(GROUPS)]
        w8_sb = keep.tile([P, M], U32, align_bytes=64)
        w4_sb = keep.tile([P, 2, 2 * M], U8, align_bytes=64)
        w8_plane = keep.tile([P, M], U8, align_bytes=64)
        w4_planes = keep.tile([P, 2 * M], U8, align_bytes=64)

        def load_x_whole(c):
            rows = x[c * SPAN : (c + 1) * SPAN, :]
            nc.sync.dma_start(out=x_whole[c][:], in_=rows.rearrange("(p j) t -> p j t", j=PACK))

        def load_x_last(a):
            rows = x[(PASSES - 1) * SPAN :, a * SPAN : (a + 1) * SPAN]
            nc.sync.dma_start(out=x_last[a][:], in_=rows.rearrange("(p j) t -> p j t", j=PACK))

        def load_g(a, u):
            rows = g[a * SPAN : (a + 1) * SPAN, :].rearrange("(p r) n -> p r n", r=PACK)
            nc.sync.dma_start(out=g_sb[a, u][:], in_=rows[:, 2 * u : 2 * u + 2, :])

        def load_scales(planes, src, first_row):
            dst = planes[:].bitcast(I32).rearrange("p (a n) -> p a n", a=src.shape[0])
            for s in range(4):
                rows = src[:, s:16:4, :].bitcast(I32).rearrange("a q n -> q a n")
                nc.sync.dma_start(out=dst[first_row + s : P : 32], in_=rows)

        def deal_views(a, c, u):
            raw = x_last[a][:] if c == PASSES - 1 else x_whole[c][:, :, a * SPAN : (a + 1) * SPAN]
            src = raw.rearrange("p j (m r) -> p m j r", r=PACK)[:, :, :, 2 * u : 2 * u + 2]
            dst = x_bf[a, c, u][:].rearrange("p (r m j) -> p m j r", r=2, j=PACK)
            return dst, src

        def round_x_vector(a, c, u):
            dst, src = deal_views(a, c, u)
            nc.vector.tensor_copy(out=dst, in_=src)

        def round_x_scalar(a, c, u):
            dst, src = deal_views(a, c, u)
            nc.scalar.copy(out=dst, in_=src)

        def quantize_x(a, c):
            for u in range(2):
                cols = slice(2 * u * P, 2 * (u + 1) * P)
                nc.vector.quantize_mx(
                    out=x_codes[a, c][:, cols].bitcast(FP8X4), scales=x_scales[a, c][:, cols], in_=x_bf[a, c, u][:]
                )

        order = [(0, 0), (0, 1), (1, 0), (1, 1), (2, 0), (3, 0), (2, 1), (3, 1)]
        acc = {}

        def multiply(a, c, tiles):
            for r, h in tiles:
                cols = slice(h * N, (h + 1) * N)
                if c == 0:
                    acc[a, r, h] = psum.tile([P, N], F32, name="acc%d%d" % (r, h))
                    rhs = w8_sb[:, cols].bitcast(FP8X4)
                    rhs_scale = w8_plane[W8_ROW:, cols]
                else:
                    rhs = w4_sb[:, c - 1, 2 * h * N : 2 * (h + 1) * N].bitcast(FP4X4)
                    rhs_scale = w4_planes[:, (c - 1) * M + h * N : (c - 1) * M + (h + 1) * N]
                nc.tensor.matmul_mx(
                    out=acc[a, r, h][:],
                    lhsT=x_codes[a, c][:, r * P : (r + 1) * P].bitcast(FP8X4),
                    lhsT_scale=x_scales[a, c][:, r * P : (r + 1) * P],
                    rhs=rhs,
                    rhs_scale=rhs_scale,
                    start=(c == 0),
                    stop=(c == PASSES - 1),
                )

        def gate(a, tiles):
            for r, h in tiles:
                cols = slice(h * N, (h + 1) * N)
                nc.vector.tensor_tensor(
                    out=o_sb[a][:, r, cols], in0=acc[a, r, h][:], in1=g_sb[a, r // 2][:, r % 2, cols], op=mybir.AluOpType.mult
                )

        def out_views(a, h):
            rows = o_sb[a][:, :, h * N : (h + 1) * N]
            if h == 0:
                return o_bf[a, h][:].rearrange("p (n r) -> p n r", r=PACK), rows.rearrange("p r n -> p n r")
            dst = o_bf[a, h][:].rearrange("p (c i r) -> p c r i", i=4, r=PACK)
            return dst, rows.rearrange("p r (c i) -> p c r i", i=4)

        def round_out_scalar(a, h):
            dst, src = out_views(a, h)
            nc.scalar.copy(out=dst, in_=src)

        def round_out_vector(a, h):
            dst, src = out_views(a, h)
            nc.vector.tensor_copy(out=dst, in_=src)

        def quantize_out(a, h):
            nc.vector.quantize_mx(
                out=o_codes[a][:, h * N : (h + 1) * N].bitcast(FP8X4),
                scales=o_scales[a][OUT_ROW[a] :, h * N : (h + 1) * N],
                in_=o_bf[a, h][:],
            )

        def store_out(a, r0, r1):
            rows = out_0[a * SPAN : (a + 1) * SPAN, :].rearrange("(p r) n -> p r n", r=PACK)
            nc.sync.dma_start(out=rows[:, r0:r1, :], in_=o_sb[a][:, r0:r1, :])

        def store_codes(a):
            nc.sync.dma_start(out=out_1[a].rearrange("p n i -> p (n i)").bitcast(I32), in_=o_codes[a][:].bitcast(I32))

        def store_scales(a, queue):
            src = o_scales[a][:].bitcast(I32)
            for s in range(4):
                queue.dma_start(out=out_2[a, s:16:4, :].bitcast(I32), in_=src[OUT_ROW[a] + s : P : 32])

        nc.vector.memset(w8_plane[:].bitcast(I32), 0)
        nc.vector.memset(w4_planes[:].bitcast(I32), 0)
        load_x_whole(0)
        nc.sync.dma_start(out=w8_sb[:].bitcast(I32), in_=w8_words[0].rearrange("p n i -> p (n i)").bitcast(I32))
        load_scales(w8_plane, w8_scales, W8_ROW)
        load_x_whole(1)
        nc.sync.dma_start(out=w4_sb[:].bitcast(I32), in_=w4_words.bitcast(I32).rearrange("a p n -> p a n"))
        load_scales(w4_planes, w4_scales, 0)
        for a in range(GROUPS):
            load_x_last(a)
            load_g(a, 0)
            load_g(a, 1)

        for c in range(PASSES - 1):
            for a in range(GROUPS):
                round_x_vector(a, c, 0)
                round_x_scalar(a, c, 1)
            for a in range(GROUPS):
                quantize_x(a, c)
            multiply(0, c, order)
        round_x_vector(0, 2, 0)
        round_x_scalar(0, 2, 1)
        quantize_x(0, 2)
        multiply(0, 2, order)
        for i, tile in enumerate(order):
            gate(0, [tile])
            multiply(1, 0, [tile])
            multiply(1, 1, [tile])
            if i == 5:
                round_out_scalar(0, 0)
        round_out_scalar(0, 1)
        store_out(0, 0, PACK)
        round_x_vector(1, 2, 0)
        round_x_vector(1, 2, 1)
        quantize_x(1, 2)
        multiply(1, 2, order)
        quantize_out(0, 0)
        gate(1, order[:2])
        quantize_out(0, 1)
        store_codes(0)
        store_scales(0, nc.sync)
        gate(1, order[2:4])
        store_out(1, 0, 2)
        gate(1, order[4:6])
        round_out_scalar(1, 0)
        gate(1, order[6:])
        store_out(1, 2, PACK)
        round_out_vector(1, 1)
        quantize_out(1, 1)
        quantize_out(1, 0)
        store_codes(1)
        store_scales(1, nc.sync)
